import numpy as np, ml_dtypes
CORES = [8,136,40,168]
N = 4
NP, NBK, TK, CAP = 2, 4, 128, 5
DEST = [[3,3,3,3],[2,2,2,3]]
def setup_inputs(rng):
    return {"x": rng.standard_normal((N, 128, NBK * TK), dtype=np.float32).astype(ml_dtypes.bfloat16), "w": (rng.standard_normal((N, 128, 128), dtype=np.float32) / 8).astype(ml_dtypes.bfloat16)}
def setup_inputs_big(rng):
    d = setup_inputs(rng)
    for k in ("x", "w"): d[k] = (d[k].astype(np.float32) * 1024.0).astype(d[k].dtype)
    return d
def setup_inputs_small(rng):
    d = setup_inputs(rng)
    for k in ("x", "w"): d[k] = (d[k].astype(np.float32) * (1 / 1024.0)).astype(d[k].dtype)
    return d
def setup_inputs_apart(rng):
    d = setup_inputs(rng)
    f = (10.0 ** rng.permutation(np.linspace(-1.5, 1.5, N))).astype(np.float32).reshape(N, 1, 1)
    for k in ("x", "w"): d[k] = (d[k].astype(np.float32) * f).astype(d[k].dtype)
    return d
def reference(x, w):
    X, W = x.astype(np.float64), w.astype(np.float64)
    y = np.full((N, 128, CAP * TK), np.nan); n = [0] * N
    for p in range(NP):
        for c in range(NBK):
            q = DEST[p][c]
            y[q][:, TK * n[q]:TK * n[q] + TK] = W[q].T @ np.maximum(W[p].T @ X[p][:, TK * c:TK * c + TK], 0.0)
            n[q] += 1
    return {"y": y.astype(ml_dtypes.bfloat16 if x.dtype != np.float64 else np.float64)}

@@ -1,0 +1,99 @@
+from concourse.mybir import AluOpType
+
+NBK, TK, CAP = 4, 128, 5
+NCH = CAP
+
+SCRATCH = {
+    "ws": ("sbuf", [128, TK], "bfloat16"),
+    "stage": ("sbuf", [128, CAP * TK], "bfloat16"),
+    "h": ("sbuf", [128, CAP * TK], "bfloat16"),
+    "zero": ("sbuf", [128, NBK * TK], "bfloat16"),
+}
+for _k in range(NCH):
+    SCRATCH["ps%d" % _k] = ("psum", [128, 512], "float32")
+SEMAPHORES = ["lw", "z", "sent"] + ["%s%d" % (n, k) for n in ("lx", "mm", "ev", "ar", "st") for k in range(NCH)]
+
+
+def _plan(dest):
+    slot, load = {}, {}
+    for p, row in enumerate(dest):
+        for c, q in enumerate(row):
+            slot[p, c] = load.get(q, 0)
+            load[q] = slot[p, c] + 1
+    sends, recvs = {}, {}
+    for p, row in enumerate(dest):
+        runs = []
+        for c, q in enumerate(row):
+            if runs and runs[-1][2] == q:
+                runs[-1][1] = c + 1
+            else:
+                runs.append([c, c + 1, q])
+        runs.sort(key=lambda r: (-load[r[2]], r[0]))
+        if len(runs) == 1 and runs[0][1] - runs[0][0] > 1:
+            c0, c1, q = runs[0]
+            mid = (c0 + c1) // 2
+            runs = [[c0, mid, q], [mid, c1, q]]
+        sends[p] = runs
+        done = 0
+        for k, (c0, c1, q) in enumerate(runs):
+            done += c1 - c0
+            recvs.setdefault(q, []).append((done, p, k, slot[p, c0], c1 - c0))
+    for q in recvs:
+        recvs[q] = [t[1:] for t in sorted(recvs[q])]
+    return sends, recvs
+
+
+def _count(mask):
+    return bin(mask).count("1")
+
+
+def rank_program(g, core, T, topo):
+    rank = T.rank_of(core)
+    if rank is None:
+        return
+    S = T.sem
+    sends, recvs = _plan(T.tables["DEST"])
+    dmaq = (g.scalar, g.sync)
+
+    g.sync.dma_start(T.ws[:], T.w[:]).then_inc(S.lw, 16)
+
+    if rank in sends:
+        chunks = sends[rank]
+        g.vector.memset(T.zero[:], 0.0).then_inc(S.z, 1)
+        for k, (c0, c1, q) in enumerate(chunks):
+            a, b = c0 * TK, c1 * TK
+            dmaq[k % 2].dma_start(T.stage[:, a:b], T.x[:, a:b]).then_inc(S["lx%d" % k], 16)
+        g.tensor.wait_ge(S.lw, 16)
+        g.vector.wait_ge(S.z, 1)
+        sent = 0
+        for k, (c0, c1, q) in enumerate(chunks):
+            a, b = c0 * TK, c1 * TK
+            ps = T["ps%d" % k]
+            g.tensor.wait_ge(S["lx%d" % k], 16)
+            g.tensor.matmul(ps[:, 0:b - a], T.ws[:], T.stage[:, a:b], True, True).then_inc(S["mm%d" % k], 1)
+            g.vector.wait_ge(S["mm%d" % k], 1)
+            g.vector.tensor_tensor(T.h[:, a:b], ps[:, 0:b - a], T.zero[:, 0:b - a], AluOpType.max).then_inc(S["ev%d" % k], 1)
+            j = [t[:2] for t in recvs[q]].index((rank, k))
+            s0 = recvs[q][j][2] * TK
+            dst = T.cores[q]
+            rid, pid = topo.addr(dst, core)
+            mask = topo.mask(core, dst)
+            g.wait_ge(S["ev%d" % k], 1)
+            g.remote_dma(T.h[:, s0:s0 + b - a], T.h[:, a:b], S["ar%d" % j], S.sent, pid, rid, mask)
+            sent += _count(mask)
+        g.wait_ge(S.sent, sent)
+        return
+
+    mine = recvs.get(rank, [])
+    g.tensor.wait_ge(S.lw, 16)
+    for j, (p, k, s, nb) in enumerate(mine):
+        a, b = s * TK, (s + nb) * TK
+        ps = T["ps%d" % j]
+        g.tensor.wait_ge(S["ar%d" % j], _count(topo.mask(T.cores[p], core)))
+        g.tensor.matmul(ps[:, 0:b - a], T.ws[:], T.h[:, a:b], True, True).then_inc(S["mm%d" % j], 1)
+        g.vector.wait_ge(S["mm%d" % j], 1)
+        g.vector.tensor_copy(T.stage[:, a:b], ps[:, 0:b - a]).then_inc(S["ev%d" % j], 1)
+        dmaq[j % 2].wait_ge(S["ev%d" % j], 1)
+        dmaq[j % 2].dma_start(T.y[:, a:b], T.stage[:, a:b]).then_inc(S["st%d" % j], 16)
+    for j in range(len(mine)):
+        dmaq[j % 2].wait_ge(S["st%d" % j], 16)

@@ -1,17 +1,20 @@
 from concourse.mybir import AluOpType
 
-NBK, TK, CAP = 4, 128, 5
+NP, NBK, TK, CAP = 2, 4, 128, 5
 NCH = CAP
 
 SCRATCH = {
-    "ws": ("sbuf", [128, TK], "bfloat16"),
+    "fw": ("sbuf", [128, 2 * TK], "bfloat16"),
     "stage": ("sbuf", [128, CAP * TK], "bfloat16"),
     "h": ("sbuf", [128, CAP * TK], "bfloat16"),
     "zero": ("sbuf", [128, NBK * TK], "bfloat16"),
 }
 for _k in range(NCH):
     SCRATCH["ps%d" % _k] = ("psum", [128, 512], "float32")
-SEMAPHORES = ["lw", "z", "sent"] + ["%s%d" % (n, k) for n in ("lx", "mm", "ev", "ar", "st") for k in range(NCH)]
+for _p in range(NP):
+    SCRATCH["rw%d" % _p] = ("sbuf", [128, 2 * TK], "bfloat16")
+    SCRATCH["pr%d" % _p] = ("psum", [128, 512], "float32")
+SEMAPHORES = ["lw", "z", "sent"] + ["%s%d" % (n, k) for n in ("lx", "mm", "ev", "ar", "st", "m1", "r1") for k in range(NCH)]
 
 
 def _plan(dest):
@@ -28,16 +31,20 @@ def _plan(dest):
                 runs[-1][1] = c + 1
             else:
                 runs.append([c, c + 1, q])
-        runs.sort(key=lambda r: (-load[r[2]], r[0]))
-        if len(runs) == 1 and runs[0][1] - runs[0][0] > 1:
-            c0, c1, q = runs[0]
-            mid = (c0 + c1) // 2
-            runs = [[c0, mid, q], [mid, c1, q]]
-        sends[p] = runs
+        main = max(runs, key=lambda r: (r[1] - r[0], -r[0]))
+        c0, c1, q = main
+        seq = [(c0, c0 + 1, q, True)]
+        others = [r for r in runs if r is not main]
+        seq += [(r[0], r[1], r[2], False) for r in others]
+        if not others and c1 - c0 > 2:
+            seq += [(c0 + 1, c1 - 1, q, False), (c1 - 1, c1, q, False)]
+        elif c1 - c0 > 1:
+            seq += [(c0 + 1, c1, q, False)]
+        sends[p] = seq
         done = 0
-        for k, (c0, c1, q) in enumerate(runs):
-            done += c1 - c0
-            recvs.setdefault(q, []).append((done, p, k, slot[p, c0], c1 - c0))
+        for k, (a, b, o, raw) in enumerate(seq):
+            done += b - a + (1 if raw else 0)
+            recvs.setdefault(o, []).append((done, p, k, slot[p, a], b - a, raw))
     for q in recvs:
         recvs[q] = [t[1:] for t in sorted(recvs[q])]
     return sends, recvs
@@ -54,43 +61,57 @@ def rank_program(g, core, T, topo):
     S = T.sem
     sends, recvs = _plan(T.tables["DEST"])
     dmaq = (g.scalar, g.sync)
+    ws = T.fw[:, 0:TK]
 
-    g.sync.dma_start(T.ws[:], T.w[:]).then_inc(S.lw, 16)
+    g.sync.dma_start(ws, T.w[:]).then_inc(S.lw, 16)
+    g.vector.memset(T.zero[:], 0.0).then_inc(S.z, 1)
 
     if rank in sends:
         chunks = sends[rank]
-        g.vector.memset(T.zero[:], 0.0).then_inc(S.z, 1)
-        for k, (c0, c1, q) in enumerate(chunks):
+        for k, (c0, c1, q, raw) in enumerate(chunks):
             a, b = c0 * TK, c1 * TK
-            dmaq[k % 2].dma_start(T.stage[:, a:b], T.x[:, a:b]).then_inc(S["lx%d" % k], 16)
+            out = T.fw[:, TK:2 * TK] if raw else T.stage[:, a:b]
+            dmaq[k % 2].dma_start(out, T.x[:, a:b]).then_inc(S["lx%d" % k], 16)
         g.tensor.wait_ge(S.lw, 16)
         g.vector.wait_ge(S.z, 1)
         sent = 0
-        for k, (c0, c1, q) in enumerate(chunks):
+        for k, (c0, c1, q, raw) in enumerate(chunks):
             a, b = c0 * TK, c1 * TK
-            ps = T["ps%d" % k]
-            g.tensor.wait_ge(S["lx%d" % k], 16)
-            g.tensor.matmul(ps[:, 0:b - a], T.ws[:], T.stage[:, a:b], True, True).then_inc(S["mm%d" % k], 1)
-            g.vector.wait_ge(S["mm%d" % k], 1)
-            g.vector.tensor_tensor(T.h[:, a:b], ps[:, 0:b - a], T.zero[:, 0:b - a], AluOpType.max).then_inc(S["ev%d" % k], 1)
             j = [t[:2] for t in recvs[q]].index((rank, k))
             s0 = recvs[q][j][2] * TK
             dst = T.cores[q]
             rid, pid = topo.addr(dst, core)
             mask = topo.mask(core, dst)
-            g.wait_ge(S["ev%d" % k], 1)
-            g.remote_dma(T.h[:, s0:s0 + b - a], T.h[:, a:b], S["ar%d" % j], S.sent, pid, rid, mask)
+            if raw:
+                g.wait_ge(S.lw, 16)
+                g.wait_ge(S["lx%d" % k], 16)
+                g.remote_dma(T["rw%d" % rank][:], T.fw[:], S["ar%d" % j], S.sent, pid, rid, mask)
+            else:
+                ps = T["ps%d" % k]
+                g.tensor.wait_ge(S["lx%d" % k], 16)
+                g.tensor.matmul(ps[:, 0:b - a], ws, T.stage[:, a:b], True, True).then_inc(S["mm%d" % k], 1)
+                g.vector.wait_ge(S["mm%d" % k], 1)
+                g.vector.tensor_tensor(T.h[:, a:b], ps[:, 0:b - a], T.zero[:, 0:b - a], AluOpType.max).then_inc(S["ev%d" % k], 1)
+                g.wait_ge(S["ev%d" % k], 1)
+                g.remote_dma(T.h[:, s0:s0 + b - a], T.h[:, a:b], S["ar%d" % j], S.sent, pid, rid, mask)
             sent += _count(mask)
         g.wait_ge(S.sent, sent)
         return
 
     mine = recvs.get(rank, [])
     g.tensor.wait_ge(S.lw, 16)
-    for j, (p, k, s, nb) in enumerate(mine):
+    g.vector.wait_ge(S.z, 1)
+    for j, (p, k, s, nb, raw) in enumerate(mine):
         a, b = s * TK, (s + nb) * TK
         ps = T["ps%d" % j]
         g.tensor.wait_ge(S["ar%d" % j], _count(topo.mask(T.cores[p], core)))
-        g.tensor.matmul(ps[:, 0:b - a], T.ws[:], T.h[:, a:b], True, True).then_inc(S["mm%d" % j], 1)
+        if raw:
+            rw, pr = T["rw%d" % p], T["pr%d" % p]
+            g.tensor.matmul(pr[:, 0:TK], rw[:, 0:TK], rw[:, TK:2 * TK], True, True).then_inc(S["m1%d" % j], 1)
+            g.vector.wait_ge(S["m1%d" % j], 1)
+            g.vector.tensor_tensor(T.h[:, a:b], pr[:, 0:TK], T.zero[:, 0:TK], AluOpType.max).then_inc(S["r1%d" % j], 1)
+            g.tensor.wait_ge(S["r1%d" % j], 1)
+        g.tensor.matmul(ps[:, 0:b - a], ws, T.h[:, a:b], True, True).then_inc(S["mm%d" % j], 1)
         g.vector.wait_ge(S["mm%d" % j], 1)
         g.vector.tensor_copy(T.stage[:, a:b], ps[:, 0:b - a]).then_inc(S["ev%d" % j], 1)
         dmaq[j % 2].wait_ge(S["ev%d" % j], 1)

from concourse.mybir import AluOpType

NP, NBK, TK, CAP = 2, 4, 128, 5
NCH = CAP

SCRATCH = {
    "fw": ("sbuf", [128, 2 * TK], "bfloat16"),
    "stage": ("sbuf", [128, CAP * TK], "bfloat16"),
    "h": ("sbuf", [128, CAP * TK], "bfloat16"),
    "zero": ("sbuf", [128, NBK * TK], "bfloat16"),
}
for _k in range(NCH):
    SCRATCH["ps%d" % _k] = ("psum", [128, 512], "float32")
for _p in range(NP):
    SCRATCH["rw%d" % _p] = ("sbuf", [128, 2 * TK], "bfloat16")
    SCRATCH["pr%d" % _p] = ("psum", [128, 512], "float32")
SEMAPHORES = ["lw", "z", "sent"] + ["%s%d" % (n, k) for n in ("lx", "mm", "ev", "ar", "st", "m1", "r1") for k in range(NCH)]


def _plan(dest):
    slot, load = {}, {}
    for p, row in enumerate(dest):
        for c, q in enumerate(row):
            slot[p, c] = load.get(q, 0)
            load[q] = slot[p, c] + 1
    sends, recvs = {}, {}
    for p, row in enumerate(dest):
        runs = []
        for c, q in enumerate(row):
            if runs and runs[-1][2] == q:
                runs[-1][1] = c + 1
            else:
                runs.append([c, c + 1, q])
        main = max(runs, key=lambda r: (r[1] - r[0], -r[0]))
        c0, c1, q = main
        seq = [(c0, c0 + 1, q, True)]
        others = [r for r in runs if r is not main]
        seq += [(r[0], r[1], r[2], False) for r in others]
        if not others and c1 - c0 > 2:
            seq += [(c0 + 1, c1 - 1, q, False), (c1 - 1, c1, q, False)]
        elif c1 - c0 > 1:
            seq += [(c0 + 1, c1, q, False)]
        sends[p] = seq
        done = 0
        for k, (a, b, o, raw) in enumerate(seq):
            done += b - a + (1 if raw else 0)
            recvs.setdefault(o, []).append((done, p, k, slot[p, a], b - a, raw))
    for q in recvs:
        recvs[q] = [t[1:] for t in sorted(recvs[q])]
    return sends, recvs


def _count(mask):
    return bin(mask).count("1")


def rank_program(g, core, T, topo):
    rank = T.rank_of(core)
    if rank is None:
        return
    S = T.sem
    sends, recvs = _plan(T.tables["DEST"])
    dmaq = (g.scalar, g.sync)
    ws = T.fw[:, 0:TK]

    g.sync.dma_start(ws, T.w[:]).then_inc(S.lw, 16)
    g.vector.memset(T.zero[:], 0.0).then_inc(S.z, 1)

    if rank in sends:
        chunks = sends[rank]
        for k, (c0, c1, q, raw) in enumerate(chunks):
            a, b = c0 * TK, c1 * TK
            out = T.fw[:, TK:2 * TK] if raw else T.stage[:, a:b]
            dmaq[k % 2].dma_start(out, T.x[:, a:b]).then_inc(S["lx%d" % k], 16)
        g.tensor.wait_ge(S.lw, 16)
        g.vector.wait_ge(S.z, 1)
        sent = 0
        for k, (c0, c1, q, raw) in enumerate(chunks):
            a, b = c0 * TK, c1 * TK
            j = [t[:2] for t in recvs[q]].index((rank, k))
            s0 = recvs[q][j][2] * TK
            dst = T.cores[q]
            rid, pid = topo.addr(dst, core)
            mask = topo.mask(core, dst)
            if raw:
                g.wait_ge(S.lw, 16)
                g.wait_ge(S["lx%d" % k], 16)
                g.remote_dma(T["rw%d" % rank][:], T.fw[:], S["ar%d" % j], S.sent, pid, rid, mask)
            else:
                ps = T["ps%d" % k]
                g.tensor.wait_ge(S["lx%d" % k], 16)
                g.tensor.matmul(ps[:, 0:b - a], ws, T.stage[:, a:b], True, True).then_inc(S["mm%d" % k], 1)
                g.vector.wait_ge(S["mm%d" % k], 1)
                g.vector.tensor_tensor(T.h[:, a:b], ps[:, 0:b - a], T.zero[:, 0:b - a], AluOpType.max).then_inc(S["ev%d" % k], 1)
                g.wait_ge(S["ev%d" % k], 1)
                g.remote_dma(T.h[:, s0:s0 + b - a], T.h[:, a:b], S["ar%d" % j], S.sent, pid, rid, mask)
            sent += _count(mask)
        g.wait_ge(S.sent, sent)
        return

    mine = recvs.get(rank, [])
    g.tensor.wait_ge(S.lw, 16)
    g.vector.wait_ge(S.z, 1)
    for j, (p, k, s, nb, raw) in enumerate(mine):
        a, b = s * TK, (s + nb) * TK
        ps = T["ps%d" % j]
        g.tensor.wait_ge(S["ar%d" % j], _count(topo.mask(T.cores[p], core)))
        if raw:
            rw, pr = T["rw%d" % p], T["pr%d" % p]
            g.tensor.matmul(pr[:, 0:TK], rw[:, 0:TK], rw[:, TK:2 * TK], True, True).then_inc(S["m1%d" % j], 1)
            g.vector.wait_ge(S["m1%d" % j], 1)
            g.vector.tensor_tensor(T.h[:, a:b], pr[:, 0:TK], T.zero[:, 0:TK], AluOpType.max).then_inc(S["r1%d" % j], 1)
            g.tensor.wait_ge(S["r1%d" % j], 1)
        g.tensor.matmul(ps[:, 0:b - a], ws, T.h[:, a:b], True, True).then_inc(S["mm%d" % j], 1)
        g.vector.wait_ge(S["mm%d" % j], 1)
        g.vector.tensor_copy(T.stage[:, a:b], ps[:, 0:b - a]).then_inc(S["ev%d" % j], 1)
        dmaq[j % 2].wait_ge(S["ev%d" % j], 1)
        dmaq[j % 2].dma_start(T.y[:, a:b], T.stage[:, a:b]).then_inc(S["st%d" % j], 16)
    for j in range(len(mine)):
        dmaq[j % 2].wait_ge(S["st%d" % j], 16)
